import numpy as np
import ml_dtypes


def mxq(x, axis, fmt="e4m3"):
    dtype, down = {"e4m3": (ml_dtypes.float8_e4m3fn, 7), "e5m2": (ml_dtypes.float8_e5m2, 14)}[fmt]
    v = np.moveaxis(np.asarray(x, np.float32).astype(ml_dtypes.bfloat16).astype(np.float64), axis, -1)
    blocks = v.reshape(v.shape[:-1] + (-1, 32))
    amax = np.abs(blocks).max(-1, keepdims=True)
    byte = np.maximum(np.where(amax > 0, np.frexp(amax)[1] - 1 + 127, 0) - down, 1)
    scale = np.exp2(byte - 127.0)
    codes = (blocks / scale).astype(np.float32).astype(dtype).astype(np.float64)
    return np.moveaxis((codes * scale).reshape(v.shape), -1, axis)


WIDE = False


def mx_kscale(k):
    if not WIDE:
        return np.ones(k)
    levels = np.array([10, -10, 5, -5, 0])
    if k % 512:
        return np.exp2(np.random.permutation(np.resize(levels, k // 32))).repeat(32)
    a = np.empty((k // 512, 16))
    for p in range(k // 512):
        a[p, :8] = np.random.permutation(np.resize(levels, 8))
        for g in range(8):
            far = levels[np.abs(levels - a[p, g]) >= 10]
            a[p, g + 8] = far[np.random.randint(len(far))]
    return np.exp2(a.ravel()).repeat(32)


def f64(x):
    return np.asarray(x).astype(np.float64)


def striped(idx):
    return np.tile(np.asarray(idx).reshape(-1, 16).T, (8, 1)).astype(np.uint16)


def unstriped(offs):
    return offs[:16].T.reshape(-1).astype(np.int64)


E2M1 = np.array([0.0, 0.5, 1.0, 1.5, 2.0, 3.0, 4.0, 6.0, -0.0, -0.5, -1.0, -1.5, -2.0, -3.0, -4.0, -6.0])


def pack_weight(w, fmt):
    k, n = w.shape
    w = f64(np.asarray(w, np.float32).astype(ml_dtypes.bfloat16)).reshape(k // 32, 32, n)
    amax = np.abs(w).max(1)
    if fmt == "e4m3":
        byte = np.frexp(amax)[1] - 1 + 127 - 7
    else:
        mant, ex = np.frexp(amax / 6.0)
        byte = np.where(mant > 0.5, ex, ex - 1) + 127
    byte = np.clip(np.where(amax > 0, byte, 1), 1, 254)
    scaled = (w * np.exp2(127.0 - byte)[:, None, :]).reshape(k, n).astype(np.float32)
    by_word = np.ascontiguousarray(scaled.reshape(k // 512, 128, 4, n).transpose(0, 1, 3, 2))
    if fmt == "e4m3":
        words = by_word.astype(ml_dtypes.float8_e4m3fn).view(np.uint8)
    else:
        c = by_word.astype(ml_dtypes.float4_e2m1fn).view(np.uint8) & 0xF
        words = (c[..., 0::2] | (c[..., 1::2] << 4)).reshape(k // 512, 128, 2 * n)
    return np.ascontiguousarray(words), np.ascontiguousarray(byte.astype(np.uint8).reshape(k // 512, 16, n))


def unpack_weight(words, scales, fmt):
    g, _, n = scales.shape
    words = np.ascontiguousarray(words).reshape(g, 128, n, -1)
    if fmt == "e4m3":
        vals = words.view(ml_dtypes.float8_e4m3fn).astype(np.float64)
    else:
        nib = np.empty((g, 128, n, 4), np.uint8)
        nib[..., 0::2] = words & 0xF
        nib[..., 1::2] = words >> 4
        vals = E2M1[nib]
    vals = vals * np.repeat(np.exp2(scales.astype(np.float64) - 127.0), 8, axis=1)[..., None]
    return vals.transpose(0, 1, 3, 2).reshape(g * 512, n)


def sigmoid(v):
    return 1.0 / (1.0 + np.exp(-v))


D, E, T, I, Q, G = 512, 512, 2048, 512, 256, 32


def setup_inputs():
    n = np.random.standard_normal
    idx = np.random.permutation(T)[:I]
    fd = mx_kscale(D)
    fi = mx_kscale(I)
    ti = np.ones(T)
    ti[idx] = fi
    keysp = pack_weight(n((D, T)) / fd[:, None], "e4m3")
    return {
        "query": (n((D, Q)) * 1.0 / np.sqrt(D) * fd[:, None]).astype(np.float32),
        "dquery": (n((D, Q)) * 1.0 / np.sqrt(D) * fd[:, None]).astype(np.float32),
        "keys_words": keysp[0],
        "keys_scales": keysp[1],
        "steep": (np.random.uniform(1.0, 4.0, (I, 1))).astype(np.float32),
        "os": (np.random.uniform(0.02, 0.1, (I, 1)) * fi[:, None]).astype(np.float32),
        "vals": (n((E, T)) / ti).astype(np.float32),
        "offs": striped(idx),
    }


def reference(query, dquery, keys_words, keys_scales, steep, os, vals, offs):
    idx = unstriped(offs)
    keysu = unpack_weight(keys_words, keys_scales, "e4m3")
    keysidxg = keysu[:, idx]
    queryq = mxq(f64(query), 0, "e4m3")
    a = keysidxg.T @ queryq
    dqueryq = mxq(f64(dquery), 0, "e4m3")
    ta = keysidxg.T @ dqueryq
    s = a.reshape(I, G, Q // G).mean(axis=2)
    sr = np.repeat(s, Q // G, axis=1)
    w = sigmoid((a - sr) * f64(steep))
    ts = ta.reshape(I, G, Q // G).mean(axis=2)
    tsr = np.repeat(ts, Q // G, axis=1)
    tw = (ta - tsr) * f64(steep) * w * (1.0 - w)
    wo1 = tw * f64(os)
    vt1 = f64(vals)[:, idx].T
    wo1q = mxq(wo1, 0, "e4m3")
    vt1q = mxq(vt1, 0, "e4m3")
    o = wo1q.T @ vt1q
    return o

@@ -1,0 +1,251 @@
+from contextlib import ExitStack
+
+import concourse.mybir as mybir
+from concourse.masks import make_identity
+
+D, E, T, I, Q, G = 512, 512, 2048, 512, 256, 32
+FLOPS = 2 * (2 * D * I * Q + I * Q * E)
+
+F32 = mybir.dt.float32
+BF16 = mybir.dt.bfloat16
+I32 = mybir.dt.int32
+U32 = mybir.dt.uint32
+U16 = mybir.dt.uint16
+U8 = mybir.dt.uint8
+FP8X4 = mybir.dt.float8_e4m3fn_x4
+ALU = mybir.AluOpType
+ACT = mybir.ActivationFunctionType
+
+P = 128
+PACK = 4
+TEAM = Q // G
+VALUE_GROUPS = ((0, 1), (2,), (3,))
+
+
+def tile_attend_ttteamcontrast_kernel(
+    tc, query, dquery, keys_words, keys_scales, steep, slot_factor, vals, offs, out
+):
+    nc = tc.nc
+    with ExitStack() as ctx:
+        keep = ctx.enter_context(tc.tile_pool(name="keep", bufs=1))
+        loads = ctx.enter_context(tc.tile_pool(name="loads", bufs=1))
+        psum = ctx.enter_context(tc.psum_pool(name="psum", bufs=1))
+
+        def load_tile(shape, dtype, name, tag):
+            return loads.tile(shape, dtype, name=name, tag=tag, align_bytes=64)
+
+        offsets = keep.tile([P, I // 16], U16, name="offsets")
+        nc.sync.dma_start(offsets[:], offs)
+
+        scale_pool = load_tile([P, T], U8, "scale_pool", "b")
+        for quad in range(4):
+            rows = keys_scales[0, 4 * quad : 4 * quad + 4, :].bitcast(I32)
+            nc.sync.dma_start(
+                scale_pool[32 * quad : 32 * (quad + 1), :].bitcast(I32),
+                rows.unsqueeze(0).to_broadcast([8, 4, T // 4]),
+            )
+        query_raw = load_tile([P, PACK, Q], F32, "query_raw", "c")
+        nc.sync.dma_start(query_raw[:], query.rearrange("(p t) q -> p t q", t=PACK))
+        word_pool = load_tile([P, T], U32, "word_pool", "a")
+        nc.sync.dma_start(
+            word_pool[:].bitcast(I32),
+            keys_words[0].rearrange("p n t -> p (n t)").bitcast(I32),
+        )
+        dquery_raw = load_tile([P, PACK, Q], F32, "dquery_raw", "e")
+        nc.sync.dma_start(dquery_raw[:], dquery.rearrange("(p t) q -> p t q", t=PACK))
+
+        steep_sb = keep.tile([P, PACK], F32, name="steep_sb")
+        nc.sync.dma_start(steep_sb[:], steep.rearrange("(p t) o -> p (t o)", t=PACK))
+        factor_sb = keep.tile([P, PACK], F32, name="factor_sb")
+        nc.sync.dma_start(factor_sb[:], slot_factor.rearrange("(p t) o -> p (t o)", t=PACK))
+        ident = keep.tile([P, P], F32, name="ident")
+        make_identity(nc, ident[:])
+
+        def load_values(block, tag):
+            pool_tile = load_tile([P, T], F32, "value_pool%d" % block, tag)
+            nc.sync.dma_start(pool_tile[:], vals[P * block : P * (block + 1), :])
+            return pool_tile
+
+        value_pools = [load_values(block, "v%d" % block) for block in range(4)]
+
+        scale_listed = keep.tile([P, I], U8, name="scale_listed", align_bytes=64)
+        nc.vector.tensor_copy(scale_listed[:], scale_pool[:].indirect(offsets[:]))
+        key_scales = keep.tile([P, I], U8, name="key_scales", align_bytes=64)
+        nc.vector.tensor_copy(
+            key_scales[:].rearrange("p (t s) -> p t s", t=PACK),
+            scale_listed[:].rearrange("p (s t) -> p t s", t=PACK),
+        )
+        key_codes = keep.tile([P, I], U32, name="key_codes", align_bytes=64)
+        nc.vector.tensor_copy(
+            key_codes[:].rearrange("p (t s) -> p s t", t=PACK),
+            word_pool[:].indirect(offsets[:]),
+        )
+
+
+        def quantize_rows(raw, name):
+            grouped = load_tile([P, Q, PACK], BF16, name + "_grouped", name + "_grouped")
+            nc.scalar.copy(
+                grouped[:].rearrange("p (c i) t -> p c t i", i=4),
+                raw[:].rearrange("p t (c i) -> p c t i", i=4),
+            )
+            codes = keep.tile([P, Q], U32, name=name + "_codes", align_bytes=64)
+            scales = keep.tile([P, Q], U8, name=name + "_scales", align_bytes=64)
+            nc.vector.quantize_mx(
+                out=codes[:].bitcast(FP8X4),
+                scales=scales[:],
+                in_=grouped[:].rearrange("p q t -> p (q t)"),
+            )
+            return codes, scales
+
+        def score_pair(codes, scales, pair, name):
+            bank = psum.tile([P, 2, Q], F32, name=name, tag="score", bufs=4)
+            for half in range(2):
+                t = 2 * pair + half
+                nc.tensor.matmul_mx(
+                    out=bank[:, half, :],
+                    lhsT=key_codes[:, P * t : P * (t + 1)].bitcast(FP8X4),
+                    lhsT_scale=key_scales[:, P * t : P * (t + 1)],
+                    rhs=codes[:].bitcast(FP8X4),
+                    rhs_scale=scales[:],
+                    start=True,
+                    stop=True,
+                )
+            return bank
+
+        grouped_early = keep.tile([P, 2 * I], BF16, name="grouped_early", align_bytes=64)
+        grouped_third = keep.tile([P, I], BF16, name="grouped_third", align_bytes=64)
+        grouped_last = keep.tile([P, I], BF16, name="grouped_last", align_bytes=64)
+        value_grouped = [grouped_early[:, :I], grouped_early[:, I:], grouped_third[:], grouped_last[:]]
+
+        def gather_values(block):
+            listed = keep.tile([P, I], BF16, name="value_listed%d" % block, align_bytes=64)
+            nc.vector.tensor_copy(listed[:], value_pools[block][:].indirect(offsets[:]))
+            words = listed[:].bitcast(F32)
+            turned = psum.tile([P, 2, P], F32, name="value_turned", tag="turn%d" % (block % 2))
+            for u in range(2):
+                nc.tensor.transpose(turned[:, u, :], words[:, u::2], ident[:])
+            nc.scalar.copy(
+                value_grouped[block].bitcast(F32).rearrange("p (e u) -> p e u", u=2),
+                turned[:].rearrange("p u e -> p e u"),
+            )
+
+        def quantize(grouped, codes, name):
+            scales = keep.tile([P, codes.shape[1]], U8, name=name, align_bytes=64)
+            nc.vector.quantize_mx(out=codes.bitcast(FP8X4), scales=scales[:], in_=grouped)
+            return codes, scales[:]
+
+        half_steep = keep.tile([P, PACK], F32, name="half_steep")
+        nc.vector.tensor_scalar(half_steep[:], steep_sb[:], 0.5, None, ALU.mult)
+        change_scale = load_tile([P, PACK], F32, "change_scale", "bent")
+        nc.vector.scalar_tensor_tensor(
+            change_scale[:], steep_sb[:], -0.25, factor_sb[:], ALU.mult, ALU.mult
+        )
+        query_codes, query_scales = quantize_rows(query_raw, "query")
+        dquery_codes, dquery_scales = quantize_rows(dquery_raw, "dquery")
+
+        a_banks = [score_pair(query_codes, query_scales, pair, "a_bank") for pair in range(2)]
+        ta_banks = [score_pair(dquery_codes, dquery_scales, pair, "ta_bank") for pair in range(2)]
+
+        a_sums = []
+        for pair in range(2):
+            sums = load_tile([P, 2 * G], F32, "a_sums%d" % pair, ("dquery_grouped", "query_grouped")[pair])
+            nc.vector.tensor_reduce(
+                sums[:],
+                a_banks[pair][:].rearrange("p t (g j) -> p (t g) j", j=TEAM),
+                mybir.AxisListType.X,
+                ALU.add,
+            )
+            a_sums.append(sums)
+        centred = []
+        for pair in range(2):
+            tile = keep.tile([P, 2, Q], F32, name="centred%d" % pair)
+            nc.vector.scalar_tensor_tensor(
+                tile[:].rearrange("p t (g j) -> p (t g) j", j=TEAM),
+                a_sums[pair][:].unsqueeze(2).to_broadcast([P, 2 * G, TEAM]),
+                -1.0 / TEAM,
+                a_banks[pair][:].rearrange("p t (g j) -> p (t g) j", j=TEAM),
+                ALU.mult,
+                ALU.add,
+            )
+            centred.append(tile)
+
+        ta_scaled = load_tile([P, TEAM, PACK, G], F32, "ta_scaled", "s")
+        for t in range(PACK):
+            nc.scalar.activation(
+                ta_scaled[:, :, t, :],
+                ta_banks[t // 2][:, t % 2, :].rearrange("p (g j) -> p j g", j=TEAM),
+                ACT.Copy,
+                scale=change_scale[:, t : t + 1],
+            )
+        ta_sums = psum.tile([P, P], F32, name="ta_sums", tag="turn0")
+        for j in range(TEAM):
+            nc.tensor.matmul(
+                ta_sums[:],
+                lhsT=ta_scaled[:, j, :, :].rearrange("p t g -> p (t g)"),
+                rhs=ident[:],
+                is_transpose=True,
+                start=(j == 0),
+                stop=(j == TEAM - 1),
+            )
+        means_turned = load_tile([P, P], F32, "means_turned", "sq")
+        nc.scalar.activation(means_turned[:], ta_sums[:], ACT.Copy, scale=1.0 / TEAM)
+        ta_means = psum.tile([P, P], F32, name="ta_means")
+        nc.tensor.transpose(ta_means[:], means_turned[:], ident[:])
+
+        bent = load_tile([P, PACK, Q], F32, "bent", "bent")
+        for t in range(PACK):
+            nc.scalar.activation(
+                bent[:, t, :], centred[t // 2][:, t % 2, :], ACT.Tanh, scale=half_steep[:, t : t + 1]
+            )
+        squared = load_tile([P, Q * PACK], F32, "squared", "sq")
+        nc.scalar.activation(
+            squared[:].rearrange("p (c i t) -> p c t i", i=4, t=PACK),
+            bent[:].rearrange("p t (c i) -> p c t i", i=4),
+            ACT.Square,
+        )
+        gather_values(0)
+        gather_values(1)
+
+        change = load_tile([P, G, TEAM, PACK], F32, "change", "v1")
+        nc.vector.tensor_tensor(
+            change[:].rearrange("p g j t -> p j g t"),
+            ta_scaled[:].rearrange("p j t g -> p j g t"),
+            ta_means[:].rearrange("p (t g) -> p g t", t=PACK).unsqueeze(1).to_broadcast([P, TEAM, G, PACK]),
+            ALU.subtract,
+        )
+        gather_values(2)
+        early_codes = load_tile([P, 2 * P], U32, "early_codes", "s")
+        value_operands = [quantize(grouped_early[:], early_codes[:], "early_scales")]
+        weights = load_tile([P, Q * PACK], BF16, "weights", "v2")
+        nc.vector.scalar_tensor_tensor(
+            weights[:],
+            squared[:],
+            -1.0,
+            change[:].rearrange("p g j t -> p (g j t)"),
+            ALU.add,
+            ALU.mult,
+        )
+        gather_values(3)
+        late_codes = load_tile([P, Q + P], U32, "late_codes", "v3")
+        weight_codes, weight_scales = quantize(weights[:], late_codes[:, :Q], "weight_scales")
+        value_operands.append(quantize(grouped_third[:], late_codes[:, Q:], "third_scales"))
+        last_codes = keep.tile([P, P], U32, name="last_codes", align_bytes=64)
+        value_operands.append(quantize(grouped_last[:], last_codes[:], "last_scales"))
+
+        out_rows = out.rearrange("(h p) e -> p h e", p=P)
+        for group, (codes, scales) in zip(VALUE_GROUPS, value_operands):
+            width = P * len(group)
+            bank = psum.tile([P, 2, width], F32, name="out_bank", tag="score", bufs=4)
+            for h in range(2):
+                nc.tensor.matmul_mx(
+                    out=bank[:, h, :],
+                    lhsT=weight_codes[:, P * h : P * (h + 1)].bitcast(FP8X4),
+                    lhsT_scale=weight_scales[:, P * h : P * (h + 1)],
+                    rhs=codes.bitcast(FP8X4),
+                    rhs_scale=scales,
+                    start=True,
+                    stop=True,
+                )
+            result = keep.tile([P, 2, width], F32, name="result%d" % group[0])
+            nc.scalar.copy(result[:], bank[:])
+            nc.sync.dma_start(out_rows[:, :, P * group[0] : P * group[0] + width], result[:])

@@ -44,20 +44,20 @@ def tile_attend_ttteamcontrast_kernel(
                 scale_pool[32 * quad : 32 * (quad + 1), :].bitcast(I32),
                 rows.unsqueeze(0).to_broadcast([8, 4, T // 4]),
             )
-        query_raw = load_tile([P, PACK, Q], F32, "query_raw", "c")
-        nc.sync.dma_start(query_raw[:], query.rearrange("(p t) q -> p t q", t=PACK))
         word_pool = load_tile([P, T], U32, "word_pool", "a")
         nc.sync.dma_start(
             word_pool[:].bitcast(I32),
             keys_words[0].rearrange("p n t -> p (n t)").bitcast(I32),
         )
+        steep_sb = keep.tile([P, PACK], F32, name="steep_sb")
+        nc.scalar.dma_start(steep_sb[:], steep.rearrange("(p t) o -> p (t o)", t=PACK))
+        factor_sb = keep.tile([P, PACK], F32, name="factor_sb")
+        nc.scalar.dma_start(factor_sb[:], slot_factor.rearrange("(p t) o -> p (t o)", t=PACK))
+        query_raw = load_tile([P, PACK, Q], F32, "query_raw", "c")
+        nc.sync.dma_start(query_raw[:], query.rearrange("(p t) q -> p t q", t=PACK))
         dquery_raw = load_tile([P, PACK, Q], F32, "dquery_raw", "e")
         nc.sync.dma_start(dquery_raw[:], dquery.rearrange("(p t) q -> p t q", t=PACK))
 
-        steep_sb = keep.tile([P, PACK], F32, name="steep_sb")
-        nc.sync.dma_start(steep_sb[:], steep.rearrange("(p t) o -> p (t o)", t=PACK))
-        factor_sb = keep.tile([P, PACK], F32, name="factor_sb")
-        nc.sync.dma_start(factor_sb[:], slot_factor.rearrange("(p t) o -> p (t o)", t=PACK))
         ident = keep.tile([P, P], F32, name="ident")
         make_identity(nc, ident[:])
 
@@ -82,9 +82,9 @@ def tile_attend_ttteamcontrast_kernel(
         )
 
 
-        def quantize_rows(raw, name):
+        def quantize_rows(raw, name, copy):
             grouped = load_tile([P, Q, PACK], BF16, name + "_grouped", name + "_grouped")
-            nc.scalar.copy(
+            copy(
                 grouped[:].rearrange("p (c i) t -> p c t i", i=4),
                 raw[:].rearrange("p t (c i) -> p c t i", i=4),
             )
@@ -113,20 +113,22 @@ def tile_attend_ttteamcontrast_kernel(
             return bank
 
         grouped_early = keep.tile([P, 2 * I], BF16, name="grouped_early", align_bytes=64)
-        grouped_third = keep.tile([P, I], BF16, name="grouped_third", align_bytes=64)
-        grouped_last = keep.tile([P, I], BF16, name="grouped_last", align_bytes=64)
-        value_grouped = [grouped_early[:, :I], grouped_early[:, I:], grouped_third[:], grouped_last[:]]
+        grouped_late = keep.tile([P, 2 * I], BF16, name="grouped_late", align_bytes=64)
 
         def gather_values(block):
-            listed = keep.tile([P, I], BF16, name="value_listed%d" % block, align_bytes=64)
+            listed = load_tile([P, I], BF16, "value_listed%d" % block, ("listed0", "listed1", "s", "v1")[block])
             nc.vector.tensor_copy(listed[:], value_pools[block][:].indirect(offsets[:]))
             words = listed[:].bitcast(F32)
-            turned = psum.tile([P, 2, P], F32, name="value_turned", tag="turn%d" % (block % 2))
-            for u in range(2):
-                nc.tensor.transpose(turned[:, u, :], words[:, u::2], ident[:])
+            return words
+
+        def turn_values(block_words, grouped, tag):
+            turned = psum.tile([P, len(block_words), 2, P], F32, name="value_turned", tag=tag)
+            for b, words in enumerate(block_words):
+                for u in range(2):
+                    nc.tensor.transpose(turned[:, b, u, :], words[:, u::2], ident[:])
             nc.scalar.copy(
-                value_grouped[block].bitcast(F32).rearrange("p (e u) -> p e u", u=2),
-                turned[:].rearrange("p u e -> p e u"),
+                grouped.bitcast(F32).rearrange("p (b e u) -> p b e u", e=P, u=2),
+                turned[:].rearrange("p b u e -> p b e u"),
             )
 
         def quantize(grouped, codes, name):
@@ -135,13 +137,13 @@ def tile_attend_ttteamcontrast_kernel(
             return codes, scales[:]
 
         half_steep = keep.tile([P, PACK], F32, name="half_steep")
-        nc.vector.tensor_scalar(half_steep[:], steep_sb[:], 0.5, None, ALU.mult)
+        nc.gpsimd.tensor_scalar(half_steep[:], steep_sb[:], 0.5, 0.0, ALU.mult, ALU.add)
         change_scale = load_tile([P, PACK], F32, "change_scale", "bent")
-        nc.vector.scalar_tensor_tensor(
-            change_scale[:], steep_sb[:], -0.25, factor_sb[:], ALU.mult, ALU.mult
-        )
-        query_codes, query_scales = quantize_rows(query_raw, "query")
-        dquery_codes, dquery_scales = quantize_rows(dquery_raw, "dquery")
+        quarter_factor = keep.tile([P, PACK], F32, name="quarter_factor")
+        nc.gpsimd.tensor_scalar(quarter_factor[:], factor_sb[:], -0.25, 0.0, ALU.mult, ALU.add)
+        nc.gpsimd.tensor_tensor(change_scale[:], steep_sb[:], quarter_factor[:], ALU.mult)
+        query_codes, query_scales = quantize_rows(query_raw, "query", nc.vector.tensor_copy)
+        dquery_codes, dquery_scales = quantize_rows(dquery_raw, "dquery", nc.scalar.copy)
 
         a_banks = [score_pair(query_codes, query_scales, pair, "a_bank") for pair in range(2)]
         ta_banks = [score_pair(dquery_codes, dquery_scales, pair, "ta_bank") for pair in range(2)]
@@ -187,7 +189,7 @@ def tile_attend_ttteamcontrast_kernel(
                 start=(j == 0),
                 stop=(j == TEAM - 1),
             )
-        means_turned = load_tile([P, P], F32, "means_turned", "sq")
+        means_turned = load_tile([P, P], F32, "means_turned", "squared0")
         nc.scalar.activation(means_turned[:], ta_sums[:], ACT.Copy, scale=1.0 / TEAM)
         ta_means = psum.tile([P, P], F32, name="ta_means")
         nc.tensor.transpose(ta_means[:], means_turned[:], ident[:])
@@ -197,14 +199,13 @@ def tile_attend_ttteamcontrast_kernel(
             nc.scalar.activation(
                 bent[:, t, :], centred[t // 2][:, t % 2, :], ACT.Tanh, scale=half_steep[:, t : t + 1]
             )
-        squared = load_tile([P, Q * PACK], F32, "squared", "sq")
+        squared = load_tile([P, Q * PACK], F32, "squared", "squared0")
         nc.scalar.activation(
             squared[:].rearrange("p (c i t) -> p c t i", i=4, t=PACK),
             bent[:].rearrange("p t (c i) -> p c t i", i=4),
             ACT.Square,
         )
-        gather_values(0)
-        gather_values(1)
+        turn_values([gather_values(0), gather_values(1)], grouped_early[:], "turn0")
 
         change = load_tile([P, G, TEAM, PACK], F32, "change", "v1")
         nc.vector.tensor_tensor(
@@ -213,39 +214,38 @@ def tile_attend_ttteamcontrast_kernel(
             ta_means[:].rearrange("p (t g) -> p g t", t=PACK).unsqueeze(1).to_broadcast([P, TEAM, G, PACK]),
             ALU.subtract,
         )
-        gather_values(2)
-        early_codes = load_tile([P, 2 * P], U32, "early_codes", "s")
-        value_operands = [quantize(grouped_early[:], early_codes[:], "early_scales")]
+        turn_values([gather_values(2)], grouped_late[:, :I], "turn1")
         weights = load_tile([P, Q * PACK], BF16, "weights", "v2")
         nc.vector.scalar_tensor_tensor(
-            weights[:],
-            squared[:],
-            -1.0,
-            change[:].rearrange("p g j t -> p (g j t)"),
-            ALU.add,
-            ALU.mult,
+            weights[:], squared[:], -1.0, change[:].rearrange("p g j t -> p (g j t)"), ALU.add, ALU.mult
         )
-        gather_values(3)
-        late_codes = load_tile([P, Q + P], U32, "late_codes", "v3")
-        weight_codes, weight_scales = quantize(weights[:], late_codes[:, :Q], "weight_scales")
-        value_operands.append(quantize(grouped_third[:], late_codes[:, Q:], "third_scales"))
-        last_codes = keep.tile([P, P], U32, name="last_codes", align_bytes=64)
-        value_operands.append(quantize(grouped_last[:], last_codes[:], "last_scales"))
+        turn_values([gather_values(3)], grouped_late[:, I:], "turn0")
+        codes = load_tile([P, Q + 2 * P], U32, "codes", "v3")
+        value_operands = [quantize(grouped_early[:], codes[:, Q:], "early_scales")]
+        weight_codes, weight_scales = quantize(weights[:], codes[:, :Q], "weight_scales")
+        late_codes = keep.tile([P, 2 * P], U32, name="late_codes", align_bytes=64)
+        value_operands.append(quantize(grouped_late[:], late_codes[:], "late_scales"))
 
-        out_rows = out.rearrange("(h p) e -> p h e", p=P)
-        for group, (codes, scales) in zip(VALUE_GROUPS, value_operands):
-            width = P * len(group)
-            bank = psum.tile([P, 2, width], F32, name="out_bank", tag="score", bufs=4)
-            for h in range(2):
-                nc.tensor.matmul_mx(
-                    out=bank[:, h, :],
-                    lhsT=weight_codes[:, P * h : P * (h + 1)].bitcast(FP8X4),
-                    lhsT_scale=weight_scales[:, P * h : P * (h + 1)],
-                    rhs=codes.bitcast(FP8X4),
-                    rhs_scale=scales,
-                    start=True,
-                    stop=True,
-                )
-            result = keep.tile([P, 2, width], F32, name="result%d" % group[0])
-            nc.scalar.copy(result[:], bank[:])
-            nc.sync.dma_start(out_rows[:, :, P * group[0] : P * group[0] + width], result[:])
+        def product(h, part):
+            value_codes, value_scales = value_operands[part]
+            bank = psum.tile([P, 2 * P], F32, name="out_bank", tag="score", bufs=4)
+            nc.tensor.matmul_mx(
+                out=bank[:],
+                lhsT=weight_codes[:, P * h : P * (h + 1)].bitcast(FP8X4),
+                lhsT_scale=weight_scales[:, P * h : P * (h + 1)],
+                rhs=value_codes.bitcast(FP8X4),
+                rhs_scale=value_scales,
+                start=True,
+                stop=True,
+            )
+            return bank
+
+        early_result = keep.tile([P, 2, 2 * P], F32, name="early_result")
+        for h in range(2):
+            nc.scalar.copy(early_result[:, h, :], product(h, 0)[:])
+        nc.sync.dma_start(out.rearrange("(h p) e -> p h e", p=P)[:, :, : 2 * P], early_result[:])
+        late_results = [keep.tile([P, 2 * P], F32, name="late_result%d" % h) for h in range(2)]
+        nc.scalar.copy(late_results[0][:], product(0, 1)[:])
+        nc.scalar.dma_start(out[:P, 2 * P :], late_results[0][:])
+        nc.vector.tensor_copy(late_results[1][:], product(1, 1)[:])
+        nc.sync.dma_start(out[P:, 2 * P :], late_results[1][:])

@@ -82,9 +82,9 @@ def tile_attend_ttteamcontrast_kernel(
         )
 
 
-        def quantize_rows(raw, name, copy):
+        def quantize_rows(raw, name):
             grouped = load_tile([P, Q, PACK], BF16, name + "_grouped", name + "_grouped")
-            copy(
+            nc.scalar.copy(
                 grouped[:].rearrange("p (c i) t -> p c t i", i=4),
                 raw[:].rearrange("p t (c i) -> p c t i", i=4),
             )
@@ -112,11 +112,10 @@ def tile_attend_ttteamcontrast_kernel(
                 )
             return bank
 
-        grouped_early = keep.tile([P, 2 * I], BF16, name="grouped_early", align_bytes=64)
         grouped_late = keep.tile([P, 2 * I], BF16, name="grouped_late", align_bytes=64)
 
         def gather_values(block):
-            listed = load_tile([P, I], BF16, "value_listed%d" % block, ("listed0", "listed1", "s", "v1")[block])
+            listed = keep.tile([P, I], BF16, name="value_listed%d" % block, align_bytes=64)
             nc.vector.tensor_copy(listed[:], value_pools[block][:].indirect(offsets[:]))
             words = listed[:].bitcast(F32)
             return words
@@ -142,28 +141,26 @@ def tile_attend_ttteamcontrast_kernel(
         quarter_factor = keep.tile([P, PACK], F32, name="quarter_factor")
         nc.gpsimd.tensor_scalar(quarter_factor[:], factor_sb[:], -0.25, 0.0, ALU.mult, ALU.add)
         nc.gpsimd.tensor_tensor(change_scale[:], steep_sb[:], quarter_factor[:], ALU.mult)
-        query_codes, query_scales = quantize_rows(query_raw, "query", nc.vector.tensor_copy)
-        dquery_codes, dquery_scales = quantize_rows(dquery_raw, "dquery", nc.scalar.copy)
+        query_codes, query_scales = quantize_rows(query_raw, "query")
+        dquery_codes, dquery_scales = quantize_rows(dquery_raw, "dquery")
 
         a_banks = [score_pair(query_codes, query_scales, pair, "a_bank") for pair in range(2)]
         ta_banks = [score_pair(dquery_codes, dquery_scales, pair, "ta_bank") for pair in range(2)]
 
-        a_sums = []
+        a_sums = load_tile([P, 2, 2 * G], F32, "a_sums", "dquery_grouped")
         for pair in range(2):
-            sums = load_tile([P, 2 * G], F32, "a_sums%d" % pair, ("dquery_grouped", "query_grouped")[pair])
             nc.vector.tensor_reduce(
-                sums[:],
+                a_sums[:, pair, :],
                 a_banks[pair][:].rearrange("p t (g j) -> p (t g) j", j=TEAM),
                 mybir.AxisListType.X,
                 ALU.add,
             )
-            a_sums.append(sums)
         centred = []
         for pair in range(2):
             tile = keep.tile([P, 2, Q], F32, name="centred%d" % pair)
             nc.vector.scalar_tensor_tensor(
                 tile[:].rearrange("p t (g j) -> p (t g) j", j=TEAM),
-                a_sums[pair][:].unsqueeze(2).to_broadcast([P, 2 * G, TEAM]),
+                a_sums[:, pair, :].unsqueeze(2).to_broadcast([P, 2 * G, TEAM]),
                 -1.0 / TEAM,
                 a_banks[pair][:].rearrange("p t (g j) -> p (t g) j", j=TEAM),
                 ALU.mult,
@@ -205,9 +202,10 @@ def tile_attend_ttteamcontrast_kernel(
             bent[:].rearrange("p t (c i) -> p c t i", i=4),
             ACT.Square,
         )
+        grouped_early = load_tile([P, 2 * I], BF16, "grouped_early", "bent")
         turn_values([gather_values(0), gather_values(1)], grouped_early[:], "turn0")
 
-        change = load_tile([P, G, TEAM, PACK], F32, "change", "v1")
+        change = keep.tile([P, G, TEAM, PACK], F32, name="change")
         nc.vector.tensor_tensor(
             change[:].rearrange("p g j t -> p j g t"),
             ta_scaled[:].rearrange("p j t g -> p j g t"),
@@ -215,7 +213,7 @@ def tile_attend_ttteamcontrast_kernel(
             ALU.subtract,
         )
         turn_values([gather_values(2)], grouped_late[:, :I], "turn1")
-        weights = load_tile([P, Q * PACK], BF16, "weights", "v2")
+        weights = keep.tile([P, Q * PACK], BF16, name="weights", align_bytes=64)
         nc.vector.scalar_tensor_tensor(
             weights[:], squared[:], -1.0, change[:].rearrange("p g j t -> p (g j t)"), ALU.add, ALU.mult
         )

@@ -38,11 +38,11 @@ def tile_attend_ttteamcontrast_kernel(
         nc.sync.dma_start(offsets[:], offs)
 
         scale_pool = load_tile([P, T], U8, "scale_pool", "b")
+        nc.gpsimd.memset(scale_pool[:].bitcast(I32), 0)
         for quad in range(4):
-            rows = keys_scales[0, 4 * quad : 4 * quad + 4, :].bitcast(I32)
             nc.sync.dma_start(
-                scale_pool[32 * quad : 32 * (quad + 1), :].bitcast(I32),
-                rows.unsqueeze(0).to_broadcast([8, 4, T // 4]),
+                scale_pool[32 * quad : 32 * quad + 4, :].bitcast(I32),
+                keys_scales[0, 4 * quad : 4 * quad + 4, :].bitcast(I32),
             )
         word_pool = load_tile([P, T], U32, "word_pool", "a")
         nc.sync.dma_start(
@@ -112,7 +112,8 @@ def tile_attend_ttteamcontrast_kernel(
                 )
             return bank
 
-        grouped_late = keep.tile([P, 2 * I], BF16, name="grouped_late", align_bytes=64)
+        grouped_third = keep.tile([P, I], BF16, name="grouped_third", align_bytes=64)
+        grouped_last = keep.tile([P, I], BF16, name="grouped_last", align_bytes=64)
 
         def gather_values(block):
             listed = keep.tile([P, I], BF16, name="value_listed%d" % block, align_bytes=64)
@@ -212,23 +213,26 @@ def tile_attend_ttteamcontrast_kernel(
             ta_means[:].rearrange("p (t g) -> p g t", t=PACK).unsqueeze(1).to_broadcast([P, TEAM, G, PACK]),
             ALU.subtract,
         )
-        turn_values([gather_values(2)], grouped_late[:, :I], "turn1")
+        turn_values([gather_values(2)], grouped_third[:], "turn1")
         weights = keep.tile([P, Q * PACK], BF16, name="weights", align_bytes=64)
         nc.vector.scalar_tensor_tensor(
             weights[:], squared[:], -1.0, change[:].rearrange("p g j t -> p (g j t)"), ALU.add, ALU.mult
         )
-        turn_values([gather_values(3)], grouped_late[:, I:], "turn0")
-        codes = load_tile([P, Q + 2 * P], U32, "codes", "v3")
-        value_operands = [quantize(grouped_early[:], codes[:, Q:], "early_scales")]
-        weight_codes, weight_scales = quantize(weights[:], codes[:, :Q], "weight_scales")
-        late_codes = keep.tile([P, 2 * P], U32, name="late_codes", align_bytes=64)
-        value_operands.append(quantize(grouped_late[:], late_codes[:], "late_scales"))
 
-        def product(h, part):
+        def quantize_new(grouped, name):
+            codes = keep.tile([P, grouped.shape[1] // PACK], U32, name=name + "_codes", align_bytes=64)
+            return quantize(grouped, codes[:], name + "_scales")
+
+        value_operands = [quantize_new(grouped_early[:], "early")]
+        weight_codes, weight_scales = quantize_new(weights[:], "weight")
+        value_operands.append(quantize_new(grouped_third[:], "third"))
+        turn_values([gather_values(3)], grouped_last[:], "turn0")
+        value_operands.append(quantize_new(grouped_last[:], "last"))
+
+        def product(h, part, bank):
             value_codes, value_scales = value_operands[part]
-            bank = psum.tile([P, 2 * P], F32, name="out_bank", tag="score", bufs=4)
             nc.tensor.matmul_mx(
-                out=bank[:],
+                out=bank,
                 lhsT=weight_codes[:, P * h : P * (h + 1)].bitcast(FP8X4),
                 lhsT_scale=weight_scales[:, P * h : P * (h + 1)],
                 rhs=value_codes.bitcast(FP8X4),
@@ -236,14 +240,18 @@ def tile_attend_ttteamcontrast_kernel(
                 start=True,
                 stop=True,
             )
-            return bank
 
-        early_result = keep.tile([P, 2, 2 * P], F32, name="early_result")
-        for h in range(2):
-            nc.scalar.copy(early_result[:, h, :], product(h, 0)[:])
-        nc.sync.dma_start(out.rearrange("(h p) e -> p h e", p=P)[:, :, : 2 * P], early_result[:])
-        late_results = [keep.tile([P, 2 * P], F32, name="late_result%d" % h) for h in range(2)]
-        nc.scalar.copy(late_results[0][:], product(0, 1)[:])
-        nc.scalar.dma_start(out[:P, 2 * P :], late_results[0][:])
-        nc.vector.tensor_copy(late_results[1][:], product(1, 1)[:])
-        nc.sync.dma_start(out[P:, 2 * P :], late_results[1][:])
+        out_rows = out.rearrange("(h p) e -> p h e", p=P)
+        for part, (first, width) in enumerate(((0, 2 * P), (2 * P, P))):
+            bank = psum.tile([P, 2, width], F32, name="out_bank", tag="score", bufs=4)
+            for h in range(2):
+                product(h, part, bank[:, h, :])
+            result = keep.tile([P, 2, width], F32, name="result%d" % part)
+            nc.scalar.copy(result[:], bank[:])
+            nc.sync.dma_start(out_rows[:, :, first : first + width], result[:])
+        for h, (copy, queue) in enumerate(((nc.scalar.copy, nc.scalar), (nc.vector.tensor_copy, nc.sync))):
+            bank = psum.tile([P, P], F32, name="last_bank", tag="score", bufs=4)
+            product(h, 2, bank[:])
+            result = keep.tile([P, P], F32, name="last_result%d" % h)
+            copy(result[:], bank[:])
+            queue.dma_start(out_rows[:, h, 3 * P :], result[:])

from contextlib import ExitStack

import concourse.mybir as mybir
from concourse.masks import make_identity

D, E, T, I, Q, G = 512, 512, 2048, 512, 256, 32
FLOPS = 2 * (2 * D * I * Q + I * Q * E)

F32 = mybir.dt.float32
BF16 = mybir.dt.bfloat16
I32 = mybir.dt.int32
U32 = mybir.dt.uint32
U16 = mybir.dt.uint16
U8 = mybir.dt.uint8
FP8X4 = mybir.dt.float8_e4m3fn_x4
ALU = mybir.AluOpType
ACT = mybir.ActivationFunctionType

P = 128
PACK = 4
TEAM = Q // G
VALUE_GROUPS = ((0, 1), (2,), (3,))


def tile_attend_ttteamcontrast_kernel(
    tc, query, dquery, keys_words, keys_scales, steep, slot_factor, vals, offs, out
):
    nc = tc.nc
    with ExitStack() as ctx:
        keep = ctx.enter_context(tc.tile_pool(name="keep", bufs=1))
        loads = ctx.enter_context(tc.tile_pool(name="loads", bufs=1))
        psum = ctx.enter_context(tc.psum_pool(name="psum", bufs=1))

        def load_tile(shape, dtype, name, tag):
            return loads.tile(shape, dtype, name=name, tag=tag, align_bytes=64)

        offsets = keep.tile([P, I // 16], U16, name="offsets")
        nc.sync.dma_start(offsets[:], offs)

        scale_pool = load_tile([P, T], U8, "scale_pool", "b")
        nc.gpsimd.memset(scale_pool[:].bitcast(I32), 0)
        for quad in range(4):
            nc.sync.dma_start(
                scale_pool[32 * quad : 32 * quad + 4, :].bitcast(I32),
                keys_scales[0, 4 * quad : 4 * quad + 4, :].bitcast(I32),
            )
        word_pool = load_tile([P, T], U32, "word_pool", "a")
        nc.sync.dma_start(
            word_pool[:].bitcast(I32),
            keys_words[0].rearrange("p n t -> p (n t)").bitcast(I32),
        )
        steep_sb = keep.tile([P, PACK], F32, name="steep_sb")
        nc.scalar.dma_start(steep_sb[:], steep.rearrange("(p t) o -> p (t o)", t=PACK))
        factor_sb = keep.tile([P, PACK], F32, name="factor_sb")
        nc.scalar.dma_start(factor_sb[:], slot_factor.rearrange("(p t) o -> p (t o)", t=PACK))
        query_raw = load_tile([P, PACK, Q], F32, "query_raw", "c")
        nc.sync.dma_start(query_raw[:], query.rearrange("(p t) q -> p t q", t=PACK))
        dquery_raw = load_tile([P, PACK, Q], F32, "dquery_raw", "e")
        nc.sync.dma_start(dquery_raw[:], dquery.rearrange("(p t) q -> p t q", t=PACK))

        ident = keep.tile([P, P], F32, name="ident")
        make_identity(nc, ident[:])

        def load_values(block, tag):
            pool_tile = load_tile([P, T], F32, "value_pool%d" % block, tag)
            nc.sync.dma_start(pool_tile[:], vals[P * block : P * (block + 1), :])
            return pool_tile

        value_pools = [load_values(block, "v%d" % block) for block in range(4)]

        scale_listed = keep.tile([P, I], U8, name="scale_listed", align_bytes=64)
        nc.vector.tensor_copy(scale_listed[:], scale_pool[:].indirect(offsets[:]))
        key_scales = keep.tile([P, I], U8, name="key_scales", align_bytes=64)
        nc.vector.tensor_copy(
            key_scales[:].rearrange("p (t s) -> p t s", t=PACK),
            scale_listed[:].rearrange("p (s t) -> p t s", t=PACK),
        )
        key_codes = keep.tile([P, I], U32, name="key_codes", align_bytes=64)
        nc.vector.tensor_copy(
            key_codes[:].rearrange("p (t s) -> p s t", t=PACK),
            word_pool[:].indirect(offsets[:]),
        )


        def quantize_rows(raw, name):
            grouped = load_tile([P, Q, PACK], BF16, name + "_grouped", name + "_grouped")
            nc.scalar.copy(
                grouped[:].rearrange("p (c i) t -> p c t i", i=4),
                raw[:].rearrange("p t (c i) -> p c t i", i=4),
            )
            codes = keep.tile([P, Q], U32, name=name + "_codes", align_bytes=64)
            scales = keep.tile([P, Q], U8, name=name + "_scales", align_bytes=64)
            nc.vector.quantize_mx(
                out=codes[:].bitcast(FP8X4),
                scales=scales[:],
                in_=grouped[:].rearrange("p q t -> p (q t)"),
            )
            return codes, scales

        def score_pair(codes, scales, pair, name):
            bank = psum.tile([P, 2, Q], F32, name=name, tag="score", bufs=4)
            for half in range(2):
                t = 2 * pair + half
                nc.tensor.matmul_mx(
                    out=bank[:, half, :],
                    lhsT=key_codes[:, P * t : P * (t + 1)].bitcast(FP8X4),
                    lhsT_scale=key_scales[:, P * t : P * (t + 1)],
                    rhs=codes[:].bitcast(FP8X4),
                    rhs_scale=scales[:],
                    start=True,
                    stop=True,
                )
            return bank

        grouped_third = keep.tile([P, I], BF16, name="grouped_third", align_bytes=64)
        grouped_last = keep.tile([P, I], BF16, name="grouped_last", align_bytes=64)

        def gather_values(block):
            listed = keep.tile([P, I], BF16, name="value_listed%d" % block, align_bytes=64)
            nc.vector.tensor_copy(listed[:], value_pools[block][:].indirect(offsets[:]))
            words = listed[:].bitcast(F32)
            return words

        def turn_values(block_words, grouped, tag):
            turned = psum.tile([P, len(block_words), 2, P], F32, name="value_turned", tag=tag)
            for b, words in enumerate(block_words):
                for u in range(2):
                    nc.tensor.transpose(turned[:, b, u, :], words[:, u::2], ident[:])
            nc.scalar.copy(
                grouped.bitcast(F32).rearrange("p (b e u) -> p b e u", e=P, u=2),
                turned[:].rearrange("p b u e -> p b e u"),
            )

        def quantize(grouped, codes, name):
            scales = keep.tile([P, codes.shape[1]], U8, name=name, align_bytes=64)
            nc.vector.quantize_mx(out=codes.bitcast(FP8X4), scales=scales[:], in_=grouped)
            return codes, scales[:]

        half_steep = keep.tile([P, PACK], F32, name="half_steep")
        nc.gpsimd.tensor_scalar(half_steep[:], steep_sb[:], 0.5, 0.0, ALU.mult, ALU.add)
        change_scale = load_tile([P, PACK], F32, "change_scale", "bent")
        quarter_factor = keep.tile([P, PACK], F32, name="quarter_factor")
        nc.gpsimd.tensor_scalar(quarter_factor[:], factor_sb[:], -0.25, 0.0, ALU.mult, ALU.add)
        nc.gpsimd.tensor_tensor(change_scale[:], steep_sb[:], quarter_factor[:], ALU.mult)
        query_codes, query_scales = quantize_rows(query_raw, "query")
        dquery_codes, dquery_scales = quantize_rows(dquery_raw, "dquery")

        a_banks = [score_pair(query_codes, query_scales, pair, "a_bank") for pair in range(2)]
        ta_banks = [score_pair(dquery_codes, dquery_scales, pair, "ta_bank") for pair in range(2)]

        a_sums = load_tile([P, 2, 2 * G], F32, "a_sums", "dquery_grouped")
        for pair in range(2):
            nc.vector.tensor_reduce(
                a_sums[:, pair, :],
                a_banks[pair][:].rearrange("p t (g j) -> p (t g) j", j=TEAM),
                mybir.AxisListType.X,
                ALU.add,
            )
        centred = []
        for pair in range(2):
            tile = keep.tile([P, 2, Q], F32, name="centred%d" % pair)
            nc.vector.scalar_tensor_tensor(
                tile[:].rearrange("p t (g j) -> p (t g) j", j=TEAM),
                a_sums[:, pair, :].unsqueeze(2).to_broadcast([P, 2 * G, TEAM]),
                -1.0 / TEAM,
                a_banks[pair][:].rearrange("p t (g j) -> p (t g) j", j=TEAM),
                ALU.mult,
                ALU.add,
            )
            centred.append(tile)

        ta_scaled = load_tile([P, TEAM, PACK, G], F32, "ta_scaled", "s")
        for t in range(PACK):
            nc.scalar.activation(
                ta_scaled[:, :, t, :],
                ta_banks[t // 2][:, t % 2, :].rearrange("p (g j) -> p j g", j=TEAM),
                ACT.Copy,
                scale=change_scale[:, t : t + 1],
            )
        ta_sums = psum.tile([P, P], F32, name="ta_sums", tag="turn0")
        for j in range(TEAM):
            nc.tensor.matmul(
                ta_sums[:],
                lhsT=ta_scaled[:, j, :, :].rearrange("p t g -> p (t g)"),
                rhs=ident[:],
                is_transpose=True,
                start=(j == 0),
                stop=(j == TEAM - 1),
            )
        means_turned = load_tile([P, P], F32, "means_turned", "squared0")
        nc.scalar.activation(means_turned[:], ta_sums[:], ACT.Copy, scale=1.0 / TEAM)
        ta_means = psum.tile([P, P], F32, name="ta_means")
        nc.tensor.transpose(ta_means[:], means_turned[:], ident[:])

        bent = load_tile([P, PACK, Q], F32, "bent", "bent")
        for t in range(PACK):
            nc.scalar.activation(
                bent[:, t, :], centred[t // 2][:, t % 2, :], ACT.Tanh, scale=half_steep[:, t : t + 1]
            )
        squared = load_tile([P, Q * PACK], F32, "squared", "squared0")
        nc.scalar.activation(
            squared[:].rearrange("p (c i t) -> p c t i", i=4, t=PACK),
            bent[:].rearrange("p t (c i) -> p c t i", i=4),
            ACT.Square,
        )
        grouped_early = load_tile([P, 2 * I], BF16, "grouped_early", "bent")
        turn_values([gather_values(0), gather_values(1)], grouped_early[:], "turn0")

        change = keep.tile([P, G, TEAM, PACK], F32, name="change")
        nc.vector.tensor_tensor(
            change[:].rearrange("p g j t -> p j g t"),
            ta_scaled[:].rearrange("p j t g -> p j g t"),
            ta_means[:].rearrange("p (t g) -> p g t", t=PACK).unsqueeze(1).to_broadcast([P, TEAM, G, PACK]),
            ALU.subtract,
        )
        turn_values([gather_values(2)], grouped_third[:], "turn1")
        weights = keep.tile([P, Q * PACK], BF16, name="weights", align_bytes=64)
        nc.vector.scalar_tensor_tensor(
            weights[:], squared[:], -1.0, change[:].rearrange("p g j t -> p (g j t)"), ALU.add, ALU.mult
        )

        def quantize_new(grouped, name):
            codes = keep.tile([P, grouped.shape[1] // PACK], U32, name=name + "_codes", align_bytes=64)
            return quantize(grouped, codes[:], name + "_scales")

        value_operands = [quantize_new(grouped_early[:], "early")]
        weight_codes, weight_scales = quantize_new(weights[:], "weight")
        value_operands.append(quantize_new(grouped_third[:], "third"))
        turn_values([gather_values(3)], grouped_last[:], "turn0")
        value_operands.append(quantize_new(grouped_last[:], "last"))

        def product(h, part, bank):
            value_codes, value_scales = value_operands[part]
            nc.tensor.matmul_mx(
                out=bank,
                lhsT=weight_codes[:, P * h : P * (h + 1)].bitcast(FP8X4),
                lhsT_scale=weight_scales[:, P * h : P * (h + 1)],
                rhs=value_codes.bitcast(FP8X4),
                rhs_scale=value_scales,
                start=True,
                stop=True,
            )

        out_rows = out.rearrange("(h p) e -> p h e", p=P)
        for part, (first, width) in enumerate(((0, 2 * P), (2 * P, P))):
            bank = psum.tile([P, 2, width], F32, name="out_bank", tag="score", bufs=4)
            for h in range(2):
                product(h, part, bank[:, h, :])
            result = keep.tile([P, 2, width], F32, name="result%d" % part)
            nc.scalar.copy(result[:], bank[:])
            nc.sync.dma_start(out_rows[:, :, first : first + width], result[:])
        for h, (copy, queue) in enumerate(((nc.scalar.copy, nc.scalar), (nc.vector.tensor_copy, nc.sync))):
            bank = psum.tile([P, P], F32, name="last_bank", tag="score", bufs=4)
            product(h, 2, bank[:])
            result = keep.tile([P, P], F32, name="last_result%d" % h)
            copy(result[:], bank[:])
            queue.dma_start(out_rows[:, h, 3 * P :], result[:])
